import numpy as np, ml_dtypes
CORES = [78,86,94,102,110,118]
N = 6
BF = ml_dtypes.bfloat16
def f(rng, *shape):
    return (rng.standard_normal(shape, dtype=np.float32) * np.exp2(rng.integers(-2, 3, shape[:-1] + (1,)))).astype(BF)
def wide(rng, *shape):
    v = f(rng, *shape).astype(np.float32); k = shape[:-2] + (1, shape[-1])
    return (v * np.exp2(rng.integers(-6, 7, k)) * (rng.random(k) > 0.0625)).astype(BF)
def gentries(a):
    return np.ascontiguousarray(a.reshape(8, 16, -1).transpose(0, 2, 1)).reshape(8, -1)
def gtable(e):
    e = np.asarray(e); return np.ascontiguousarray(e.reshape(8, -1, 16).transpose(0, 2, 1)).reshape(128, -1).astype(np.int32)
E, S, D, F, R, V = 1536, 288, 80, 3, 3, 16384
W = E + (N - 1) * S
def arrive(a, snd):
    out = []
    for r in range(N):
        part = [a[r]]
        for t in range(1, N):
            q = (r + t) % N; p = gentries(snd[q]).reshape(8, N - 1, S)[:, N - 1 - t]
            part.append(np.take_along_axis(a[q], p[:, None, :], axis=2))
        out.append(np.concatenate(part, axis=2))
    return np.stack(out)
def slots(rng, lo, hi):
    return np.stack([rng.permuted(np.tile(np.arange(lo, hi), (8 * (N - 1), 1)), axis=1)[:, :S].reshape(8, N - 1, S) for r in range(N)])
def preds(rng):
    v = np.where(rng.random((N, 8, F, E)) < 0.5, rng.integers(0, E, (N, 8, F, E)), rng.integers(E, W, (N, 8, F, E)))
    v[:, :, 1] = np.where(rng.random((N, 8, E)) < 0.0625, v[:, :, 0], v[:, :, 1]); return v
def nodes(rng):
    return rng.integers(0, V, (N, 8, E))
def codes(rng):
    return rng.integers(0, D, (N, 8, E))
def make(rng, v, p, s, c):
    snd = np.stack([gtable(p[r].reshape(8, -1)) for r in range(N)]); a = arrive(s[:, :, None, :], snd)
    sf = np.take_along_axis(a, v.reshape(N, 8, 1, F * E), axis=3).reshape(N, 8, F, E)
    d = np.take_along_axis(sf, rng.integers(0, F, (N, 8, 1, E)), axis=2)[:, :, 0]; u = rng.integers(0, 8, (N, 8, E))
    d = np.where(u < 5, d, np.where(u < 7, d ^ 1, rng.integers(0, V, (N, 8, E))))
    return {"x": f(rng, N, 128, E), "tab": (rng.random((N, 128, D * D), dtype=np.float32) * 2 - 1).astype(BF), "dirs": c.astype(np.int32), "srcs": s.astype(np.int32), "dsts": d.astype(np.int32),
            "nb": np.stack([gtable(v[r].reshape(8, -1)) for r in range(N)]), "snd": snd}
def setup_inputs(rng):
    return make(rng, preds(rng), slots(rng, 0, E), nodes(rng), codes(rng))
def setup_inputs_ends(rng):
    p = slots(rng, 1, E - 1); p[..., 0] = E - 1; p[..., S - 1] = 0
    v = np.where(rng.random((N, 8, F, E)) < 0.75, rng.choice(np.array([0, 1, E - 1, E, E + S - 1, E + S, W - S, W - 1]), (N, 8, F, E)), preds(rng))
    return make(rng, v, p, rng.choice(np.array([0, 1, V - 2, V - 1]), (N, 8, E)), rng.choice(np.array([0, 1, D - 2, D - 1]), (N, 8, E)))
def setup_inputs_back(rng):
    s = 2 * rng.integers(0, V // 2, (1, 8, 1)) + rng.integers(0, 2, (N, 8, E))
    return make(rng, preds(rng), slots(rng, 0, E), s, codes(rng))
def setup_inputs_far(rng):
    v = rng.integers(E, W, (N, 8, F, E)); a = rng.permutation(N); t = int(rng.integers(0, N - 1))
    v[a[0]] = E + t * S + rng.integers(0, S, (8, F, E)); v[a[1]] = rng.integers(0, E, (8, F, E))
    p = slots(rng, 0, E); p[:] = p[:, :, :1].copy()
    return make(rng, v, p, nodes(rng), codes(rng))
def setup_inputs_alike(rng):
    v = preds(rng); v[:] = v[:, :, :1].copy()
    c = np.broadcast_to(rng.integers(0, D, (N, 8, 1)), (N, 8, E))
    return make(rng, v, slots(rng, 0, E), nodes(rng), c)
def setup_inputs_spread(rng):
    d = setup_inputs(rng); d["x"] = wide(rng, N, 128, E); return d
def check_inputs(d):
    bad = []
    for name, top in (("nb", W), ("snd", E), ("dirs", D), ("srcs", V), ("dsts", V)):
        if not ((d[name] >= 0) & (d[name] < top)).all(): bad.append(name + " in its range")
    p = np.stack([gentries(d["snd"][r]).reshape(8 * (N - 1), S) for r in range(N)])
    if not (np.diff(np.sort(p, axis=2), axis=2) > 0).all(): bad.append("different edges in the slots of a pair and group")
    if not (np.abs(d["x"].astype(np.float64)) <= 2.0 ** 40).all(): bad.append("x finite and at most 2**40 in size")
    if not (np.abs(d["tab"].astype(np.float64)) <= 1).all(): bad.append("tab at most 1 in size")
    return bad
def reference(x, tab, dirs, srcs, dsts, nb, snd):
    xs = x.astype(np.float64).reshape(N, 8, 16, E); v = np.stack([gentries(nb[r]) for r in range(N)])
    df = np.take_along_axis(arrive(dirs[:, :, None, :], snd)[:, :, 0], v, axis=2)
    sf = np.take_along_axis(arrive(srcs[:, :, None, :], snd)[:, :, 0], v, axis=2)
    off = D * df + np.tile(dirs, (1, 1, F)); back = sf == np.tile(dsts, (1, 1, F))
    w = []
    for r in range(N):
        c = np.take_along_axis(tab[r].astype(np.float64).reshape(8, 16, D * D), off[r][:, None, :], axis=2)
        w.append(np.where(back[r][:, None, :], 0.0, c * 0.25))
    m = xs
    for k in range(R):
        a = arrive(m, snd); new = []
        for r in range(N):
            term = w[r] * np.take_along_axis(a[r], v[r][:, None, :], axis=2)
            new.append(np.maximum(xs[r] + np.sum(term.reshape(8, 16, F, E), axis=2), 0.0))
        m = np.stack(new)
    return {"y": m.reshape(N, 128, E).astype(np.float32)}

from concourse.bass import DstId, RemoteDMATransfer
from concourse.mybir import AluOpType, ActivationFunctionType

N, E, S, D, F = 6, 1536, 288, 80, 3
W = E + (N - 1) * S
NS = (N - 1) * S
EC = E // 16
SC = S // 16
ZERO = D * D
CHUNKS = [(0, 512), (512, 1024), (1024, 1280), (1280, 1536)]
TAB_CUTS = [0, 1280, 3200, D * D]

SCRATCH = {
    "craw": ("sbuf", [128, 3 * EC], "int32"),
    "ctmp": ("sbuf", [128, 4 * EC], "int32"),
    "cb": ("sbuf", [128, 5 * EC], "bfloat16"),
    "sndr": ("sbuf", [128, NS // 16], "int32"),
    "snd16": ("sbuf", [128, NS // 16], "uint16"),
    "nbr": ("sbuf", [128, F * EC], "int32"),
    "nb16": ("sbuf", [128, F * EC], "uint16"),
    "off16": ("sbuf", [128, F * EC], "uint16"),
    "xwin": ("sbuf", [128, W], "bfloat16"),
    "mwin": ("sbuf", [128, W], "bfloat16"),
    "own2": ("sbuf", [128, E], "bfloat16"),
    "win1": ("sbuf", [128, W], "float32"),
    "win2": ("sbuf", [128, W], "float32"),
    "sx": ("sbuf", [128, NS], "bfloat16"),
    "sm": ("sbuf", [128, NS], "bfloat16"),
    "s1": ("sbuf", [128, NS], "float32"),
    "s2": ("sbuf", [128, NS], "float32"),
    "tabw": ("sbuf", [128, D * D + 16], "bfloat16"),
    "gm": ("sbuf", [128, F * E], "bfloat16"),
    "xg0": ("sbuf", [128, E], "float32"),
    "xg12": ("sbuf", [128, 2 * E], "bfloat16"),
    "w0": ("sbuf", [128, E], "float32"),
    "w12": ("sbuf", [128, 2 * E], "bfloat16"),
    "g12": ("sbuf", [128, 2 * E], "float32"),
    "prod": ("sbuf", [128, F * E], "float32"),
    "ybuf": ("sbuf", [128, E], "float32"),
    "bsel": ("sbuf", [128, 144], "bfloat16"),
    "idf": ("sbuf", [128, 128], "float32"),
    "idb": ("sbuf", [128, 128], "bfloat16"),
    "idq": ("sbuf", [128, 128], "bfloat16"),
    "zoi": ("sbuf", [128, EC], "int32"),
    "e16": ("sbuf", [128, EC], "int32"),
    "dst8": ("sbuf", [128, 2 * EC], "float32"),
    "ti": ("sbuf", [128, F * EC], "int32"),
    "lo": ("sbuf", [128, F * EC], "int32"),
    "fwd": ("sbuf", [128, F * EC], "float32"),
    "um": ("sbuf", [128, F * EC], "float32"),
    "pa": ("psum", [128, 512], "float32"),
    "pb": ("psum", [128, 512], "float32"),
    "wb0": ("psum", [128, 512], "float32"),
    "wb1": ("psum", [128, 512], "float32"),
    "wb2": ("psum", [128, 512], "float32"),
    "wb3": ("psum", [128, 512], "float32"),
    "wb4": ("psum", [128, 512], "float32"),
    "wb5": ("psum", [128, 512], "float32"),
}
SEMAPHORES = ["cv", "cs", "ct", "cg", "ldc", "lds", "ldx", "ldn", "tb", "rl1", "rl2", "st",
              "ax", "am", "a1", "a2", "lx", "lm", "l1", "l2"]


def rank_program(g, core, T, topo):
    rank = T.rank_of(core)
    if rank is None:
        return
    A, ACT = AluOpType, ActivationFunctionType
    V, SC_, PE, SY = g.vector, g.scalar, g.tensor, g.sync
    queue = {"v": V, "s": SC_, "t": PE, "y": SY, "g": g}
    count = {}
    waited = {}

    def need(q, *toks):
        best = {}
        for t in toks:
            if t is not None and t[1] > best.get(t[0], 0):
                best[t[0]] = t[1]
        for name in best:
            if waited.get((q, name), 0) < best[name]:
                queue[q].wait_ge(T.sem[name], best[name])
                waited[(q, name)] = best[name]

    def mark(ins, name, n):
        ins.then_inc(T.sem[name], n)
        count[name] = count.get(name, 0) + n
        return (name, count[name])

    def v(ins):
        return mark(ins, "cv", 1)

    def s(ins):
        return mark(ins, "cs", 1)

    def pe(ins):
        return mark(ins, "ct", 1)

    def gp(ins):
        return mark(ins, "cg", 1)

    def dma(q, out, in_, name):
        return mark(queue[q].dma_start(out, in_), name, 16)

    dma("y", T.craw[:, 0:EC], T.srcs[:], "ldc")
    dma("s", T.craw[:, 2 * EC:3 * EC], T.dirs[:], "ldc")
    ldc = dma("s", T.craw[:, EC:2 * EC], T.dsts[:], "ldc")
    lds = dma("y", T.sndr[:], T.snd[:], "lds")
    ldx = dma("y", T.xwin[:, 0:E], T.x[:], "ldx")
    ldn = dma("y", T.nbr[:], T.nb[:], "ldn")
    dma("y", T.tabw[:, TAB_CUTS[0]:TAB_CUTS[1]], T.tab[:, TAB_CUTS[0]:TAB_CUTS[1]], "tb")

    t = gp(g.iota(T.bsel[:], [[0, 144]], 16, 0, allow_small_or_imprecise_dtypes=True))
    for pat, op, fill, base, cm in (([[-16, 9], [0, 16]], A.not_equal, 80.0, 0, 1),
                                    ([[-16, 9], [0, 16]], A.is_ge, 0.0, 0, 1),
                                    ([[16, 9], [0, 16]], A.is_ge, 0.0, 15, -1),
                                    ([[0, 9], [1, 16]], A.is_equal, 0.0, -15, 0)):
        need("g", t)
        t = gp(g.affine_select(T.bsel[:], T.bsel[:], pat, op, fill, base, cm))
    bsel = t

    z_m = v(V.memset(T.mwin[:, 0:E], 0.0))
    z_o = v(V.memset(T.own2[:], 0.0))
    z_t = v(V.memset(T.tabw[:, ZERO:ZERO + 16], 0.0))

    need("v", ldc)
    v(V.tensor_scalar(T.ctmp[:, 0:2 * EC], T.craw[:, 0:2 * EC], 0x3F80, None, A.bitwise_and))
    h2 = v(V.tensor_scalar(T.ctmp[:, 2 * EC:4 * EC], T.craw[:, 0:2 * EC], 0x7F, None, A.bitwise_and))
    c_dir = v(V.tensor_copy(T.cb[:, 4 * EC:5 * EC], T.craw[:, 2 * EC:3 * EC]))
    need("v", h2)
    c_src = v(V.tensor_scalar(T.cb[:, 0:4 * EC], T.ctmp[:], 512.0, None, A.mult))
    need("v", lds)
    snd16 = v(V.tensor_copy(T.snd16[:], T.sndr[:]))
    need("y", c_dir, z_m, z_o)
    dma("y", T.mwin[0::16, 0:E], T.cb[:, 4 * EC:5 * EC], "rl1")
    dma("y", T.own2[3::16, :], T.cb[:, 4 * EC:5 * EC], "rl2")
    need("y", c_src)
    dma("y", T.mwin[1::16, 0:E], T.cb[:, 0:EC], "rl1")
    rl1 = dma("y", T.mwin[2::16, 0:E], T.cb[:, 2 * EC:3 * EC], "rl1")
    dma("y", T.own2[1::16, :], T.cb[:, EC:2 * EC], "rl2")
    rl2 = dma("y", T.own2[2::16, :], T.cb[:, 3 * EC:4 * EC], "rl2")
    dma("y", T.tabw[:, TAB_CUTS[1]:TAB_CUTS[2]], T.tab[:, TAB_CUTS[1]:TAB_CUTS[2]], "tb")

    def exchange(win, buf, ready, relu, arr, loc):
        half_a = SC // 2 + SC // 2 % 2
        mid = SC + (N - 1) // 2 * SC

        def vg(a, b):
            src = win[:, 0:E].indirect(T.snd16[:, a:b])
            if relu:
                return v(V.tensor_scalar(buf[:, 16 * a:16 * b], src, 0.0, None, A.max))
            return v(V.tensor_copy(buf[:, 16 * a:16 * b], src))

        def sg(a, b):
            src = win[:, 0:E].indirect(T.snd16[:, a:b])
            return s(SC_.activation(buf[:, 16 * a:16 * b], src, ACT.Relu if relu else ACT.Copy))

        need("v", snd16, *ready)
        need("s", snd16, *ready)
        v1, s1 = vg(0, half_a), sg(half_a, SC)
        v2, s2 = vg(SC, mid), sg(mid, NS // 16)
        total = 0
        for ts, toks in (([1], (v1, s1)), (list(range(2, N)), (v2, s2))):
            need("g", *toks)
            trs = []
            for i, tt in enumerate(ts):
                dst = T.cores[(rank + tt) % N]
                eng = topo.engines(core, dst)
                k = len(eng) // len(ts)
                mask = sum(1 << e for e in eng[i * k:(i + 1) * k])
                rid, pid = topo.addr(dst)[0:2]
                at = E + (N - tt - 1) * S
                trs.append(RemoteDMATransfer(dst_ids=[DstId(rid=rid, pnc=pid)], dma_engine_mask=mask,
                                             remote_sem=T.sem[arr], src=buf[:, (tt - 1) * S:tt * S],
                                             dst=win[:, at:at + S]))
                total += k
            g.remote_dma_fused(trs, local_sem=T.sem[loc])
        count[loc] = total
        got = 0
        for tt in range(1, N):
            got += len(topo.engines(T.cores[(rank - tt) % N], core)) // (1 if tt == 1 else N - 2)
        count[arr] = got
        return (arr, got), (loc, total), v2, s2

    ax, lx, _, _ = exchange(T.xwin, T.sx, [ldx], False, "ax", "lx")
    need("v", ldn)
    nb16 = v(V.tensor_copy(T.nb16[:], T.nbr[:]))

    am, lm, _, _ = exchange(T.mwin, T.sm, [rl1], False, "am", "lm")
    need("y", lm)
    tab = dma("y", T.tabw[:, TAB_CUTS[2]:TAB_CUTS[3]], T.tab[:, TAB_CUTS[2]:TAB_CUTS[3]], "tb")

    t = gp(g.iota(T.idf[:], [[0, 128]], 1, 0, allow_small_or_imprecise_dtypes=True))
    need("g", t)
    idf = gp(g.affine_select(T.idf[:], T.idf[:], [[-1, 128]], A.is_equal, 0.0, 0, 1))
    need("s", idf)
    idq = s(SC_.activation(T.idq[:], T.idf[:], ACT.Copy, scale=0.25))
    idb = s(SC_.activation(T.idb[:], T.idf[:], ACT.Copy))

    def wrap(out, rows, at):
        for h in range(16):
            t = pe(PE.matmul(out, T.bsel[:, 15 - h:143 - h], rows[:, at + h:at + E:16], h == 0, h == 15))
        return t

    need("t", bsel, rl2)
    zo = wrap(T.pb[:, 0:EC], T.own2, 0)
    need("v", zo)
    t = v(V.tensor_copy(T.zoi[:], T.pb[:, 0:EC]))
    need("v", t)
    e16 = v(V.tensor_scalar(T.e16[:], T.zoi[:], 8191, None, A.bitwise_and))
    need("v", e16)
    v(V.tensor_tensor(T.dst8[:, 0:EC], T.pb[:, 0:EC], T.e16[:], A.subtract))
    v(V.tensor_tensor(T.dst8[:, EC:2 * EC], T.pb[:, 0:EC], T.e16[:], A.subtract))
    for out in (T.pa[:, 2 * EC:3 * EC], T.pa[:, 3 * EC:4 * EC], T.pb[:, EC:2 * EC]):
        own = v(V.tensor_scalar(out, T.e16[:], 1.0 / 16, float(ZERO), A.mult, A.subtract))

    wb = [T["wb%d" % j] for j in range(6)]

    def to_psum(src, js):
        for j in js:
            t = pe(PE.matmul(wb[j][:], T.idq[:], src[:, 512 * j:512 * j + 512], True, True))
        return t

    need("v", ax, nb16)
    xg0 = v(V.tensor_scalar(T.xg0[:], T.xwin[:].indirect(T.nb16[:, 0:EC]), 0.25, None, A.mult))
    need("s", ax, nb16)
    xg1 = s(SC_.activation(T.xg12[:, 0:E], T.xwin[:].indirect(T.nb16[:, EC:2 * EC]), ACT.Copy))
    need("t", xg1, idq)
    to_psum(T.xg12, [0, 1, 2])
    need("v", am, own)
    need("s", am)
    zt = []
    for c in range(F):
        a, m, b = c * EC, c * EC + EC // 2, (c + 1) * EC
        t1 = v(V.tensor_copy(T.gm[:, 16 * a:16 * m], T.mwin[:].indirect(T.nb16[:, a:m])))
        t2 = s(SC_.activation(T.gm[:, 16 * m:16 * b], T.mwin[:].indirect(T.nb16[:, m:b]), ACT.Copy))
        need("t", t1, t2, own)
        zt.append(wrap(T.pa[:, a:b] if c < 2 else T.pb[:, 0:EC], T.gm, c * E))
    xg2 = s(SC_.activation(T.xg12[:, E:2 * E], T.xwin[:].indirect(T.nb16[:, 2 * EC:3 * EC]), ACT.Copy))
    need("t", xg2)
    moved = to_psum(T.xg12, [3, 4, 5])

    def offsets(bank, a, b, ready):
        n = b - a
        z, de = bank[:, 0:n], bank[:, n:2 * n]
        need("v", ready)
        t1 = v(V.tensor_tensor(T.ti[:, a:b], z, T.dst8[:, 0:n], A.subtract))
        need("v", t1)
        t2 = v(V.tensor_scalar(T.lo[:, a:b], T.ti[:, a:b], 8191, None, A.bitwise_and))
        need("v", t2)
        v(V.tensor_tensor(de, de, T.lo[:, a:b], A.add))
        t4 = v(V.tensor_tensor(T.fwd[:, a:b], T.ti[:, a:b], T.lo[:, a:b], A.not_equal))
        need("v", t4)
        t5 = v(V.tensor_tensor(T.um[:, a:b], de, T.fwd[:, a:b], A.mult))
        need("v", t5)
        return v(V.tensor_scalar(T.off16[:, a:b], T.um[:, a:b], float(ZERO), None, A.add))

    off01 = offsets(T.pa, 0, 2 * EC, zt[1])
    off2 = offsets(T.pb, 2 * EC, 3 * EC, zt[2])

    def one_round(win, lst, fac0, gbuf, out, v_ready, s_ready, free, last):
        nk = len(CHUNKS)
        banks = [T.pa, T.pb]
        gt, p0, p1, p2, acc, sm = {}, {}, {}, {}, {}, {}

        def cols(c, k):
            return lst[:, c * EC + CHUNKS[k][0] // 16:c * EC + CHUNKS[k][1] // 16]

        def s_gather(c, k):
            a, b = CHUNKS[k]
            need("s", *s_ready[c - 1])
            gt[(c, k)] = s(SC_.activation(gbuf[:, (c - 1) * E + a:(c - 1) * E + b], win.indirect(cols(c, k)), ACT.Copy))

        def v_fused(k):
            a, b = CHUNKS[k]
            p0[k] = v(V.tensor_tensor(T.prod[:, a:b], win.indirect(cols(0, k)), fac0[:, a:b], A.mult))

        def v_mult(c, k):
            a, b = CHUNKS[k]
            need("v", gt[(c, k)], v_ready[c])
            bank = wb[3 * (c - 1) + a // 512]
            t = v(V.tensor_tensor(T.prod[:, c * E + a:c * E + b], gbuf[:, (c - 1) * E + a:(c - 1) * E + b],
                                  bank[:, a % 512:a % 512 + b - a], A.mult))
            (p1 if c == 1 else p2)[k] = t

        def pe_sum(k):
            a, b = CHUNKS[k]
            o = banks[k % 2][:, 0:b - a]
            need("t", idb, free[k] if k < 2 else sm[k - 2])
            pe(PE.matmul(o, T.idb[:], T.xwin[:, a:b], True, False))
            need("t", p0[k])
            pe(PE.matmul(o, T.idf[:], T.prod[:, a:b], False, False))
            need("t", p1[k])
            acc[k] = pe(PE.matmul(o, T.idf[:], T.prod[:, E + a:E + b], False, True))

        def v_sum(k):
            a, b = CHUNKS[k]
            need("v", acc[k], p2[k])
            sm[k] = v(V.tensor_tensor(out[:, a:b], banks[k % 2][:, 0:b - a], T.prod[:, 2 * E + a:2 * E + b], A.add))

        def finish(k):
            a, b = CHUNKS[k]
            need("s", sm[k])
            t = s(SC_.activation(out[:, a:b], out[:, a:b], ACT.Relu))
            need("y", t)
            dma("y", T.y[:, a:b], out[:, a:b], "st")

        for k in range(nk):
            s_gather(1, k)
            s_gather(2, k)
        need("v", *v_ready[0])
        v_fused(0)
        v_mult(1, 0)
        pe_sum(0)
        for k in range(nk):
            if k + 1 < nk:
                v_fused(k + 1)
            v_mult(2, k)
            if k + 1 < nk and k + 2 >= nk:
                v_mult(1, k + 1)
                pe_sum(k + 1)
            v_sum(k)
            if k + 2 < nk:
                v_mult(1, k + 1)
                pe_sum(k + 1)
        if last:
            for k in range(nk):
                finish(k)
        return sm[nk - 2], sm[nk - 1], gt[(2, nk - 1)]

    tabwin = T.tabw[:]
    fa, fb, wg = one_round(tabwin, T.off16, T.xg0, T.w12, T.win1,
                           [[tab, z_t, off01, xg0], moved, moved], [[tab, z_t, off01], [off2]],
                           [off01, off2], False)
    a1, l1, v2, s2 = exchange(T.win1, T.s1, [fb], True, "a1", "l1")
    w0 = v(V.tensor_scalar(T.w0[:], tabwin.indirect(T.off16[:, 0:EC]), 0.25, None, A.mult))
    need("t", fb, wg)
    moved = to_psum(T.w12, range(6))
    need("s", v2, s2)
    r1 = s(SC_.activation(T.win1[:, 0:E], T.win1[:, 0:E], ACT.Relu))
    fa, fb, _ = one_round(T.win1[:], T.nb16, T.w0, T.g12, T.win2,
                          [[a1, r1, w0], moved, moved], [[a1, r1], []], [fa, fb], False)
    a2, l2, v2, s2 = exchange(T.win2, T.s2, [fb], True, "a2", "l2")
    need("s", v2, s2)
    r2 = s(SC_.activation(T.win2[:, 0:E], T.win2[:, 0:E], ACT.Relu))
    one_round(T.win2[:], T.nb16, T.w0, T.g12, T.ybuf,
              [[a2, r2], None, None], [[a2, r2], []], [fa, fb], True)

    for name in count:
        need("g", (name, count[name]))
